import numpy as np
import ml_dtypes


def mxq(x, axis, fmt="e4m3"):
    dtype, down = {"e4m3": (ml_dtypes.float8_e4m3fn, 7), "e5m2": (ml_dtypes.float8_e5m2, 14)}[fmt]
    v = np.moveaxis(np.asarray(x, np.float32).astype(ml_dtypes.bfloat16).astype(np.float64), axis, -1)
    blocks = v.reshape(v.shape[:-1] + (-1, 32))
    amax = np.abs(blocks).max(-1, keepdims=True)
    byte = np.maximum(np.where(amax > 0, np.frexp(amax)[1] - 1 + 127, 0) - down, 1)
    scale = np.exp2(byte - 127.0)
    codes = (blocks / scale).astype(np.float32).astype(dtype).astype(np.float64)
    return np.moveaxis((codes * scale).reshape(v.shape), -1, axis)


WIDE = False


def mx_kscale(k):
    if not WIDE:
        return np.ones(k)
    levels = np.array([10, -10, 5, -5, 0])
    if k % 512:
        return np.exp2(np.random.permutation(np.resize(levels, k // 32))).repeat(32)
    a = np.empty((k // 512, 16))
    for p in range(k // 512):
        a[p, :8] = np.random.permutation(np.resize(levels, 8))
        for g in range(8):
            far = levels[np.abs(levels - a[p, g]) >= 10]
            a[p, g + 8] = far[np.random.randint(len(far))]
    return np.exp2(a.ravel()).repeat(32)


BF16 = ml_dtypes.bfloat16


def bf(x):
    return np.asarray(x, np.float32).astype(BF16)


def f64(x):
    return np.asarray(x).astype(np.float64)


E2M1 = np.array([0.0, 0.5, 1.0, 1.5, 2.0, 3.0, 4.0, 6.0, -0.0, -0.5, -1.0, -1.5, -2.0, -3.0, -4.0, -6.0])


def pack_weight(w, fmt):
    k, n = w.shape
    w = f64(bf(w)).reshape(k // 32, 32, n)
    amax = np.abs(w).max(1)
    if fmt == "e4m3":
        byte = np.frexp(amax)[1] - 1 + 127 - 7
    else:
        mant, ex = np.frexp(amax / 6.0)
        byte = np.where(mant > 0.5, ex, ex - 1) + 127
    byte = np.clip(np.where(amax > 0, byte, 1), 1, 254)
    scaled = (w * np.exp2(127.0 - byte)[:, None, :]).reshape(k, n).astype(np.float32)
    by_word = np.ascontiguousarray(scaled.reshape(k // 512, 128, 4, n).transpose(0, 1, 3, 2))
    if fmt == "e4m3":
        words = by_word.astype(ml_dtypes.float8_e4m3fn).view(np.uint8)
    else:
        c = by_word.astype(ml_dtypes.float4_e2m1fn).view(np.uint8) & 0xF
        words = c[..., 0::2] | (c[..., 1::2] << 4)
    return np.ascontiguousarray(words), np.ascontiguousarray(byte.astype(np.uint8).reshape(k // 512, 16, n))


def unpack_weight(words, scales, fmt):
    g, p, n, _ = words.shape
    if fmt == "e4m3":
        vals = np.ascontiguousarray(words).view(ml_dtypes.float8_e4m3fn).astype(np.float64)
    else:
        nib = np.empty((g, p, n, 4), np.uint8)
        nib[..., 0::2] = words & 0xF
        nib[..., 1::2] = words >> 4
        vals = E2M1[nib]
    vals = vals * np.repeat(np.exp2(scales.astype(np.float64) - 127.0), 8, axis=1)[..., None]
    return vals.transpose(0, 1, 3, 2).reshape(g * 512, n)

E4M3FN = np.array([(-1.0 if i & 128 else 1.0) * ((1.0 + (i & 7) / 8.0) * 2.0 ** (((i >> 3) & 15) - 7) if i & 120 else (i & 7) * 2.0 ** -9) for i in range(256)])


def e4m3fn_bytes(y):
    return np.clip(np.asarray(y, np.float64), -448.0, 448.0).astype(np.float32).astype(ml_dtypes.float8_e4m3fn).view(np.uint8)


def e4m3fn_values(b):
    return E4M3FN[b]


B, D, K, N = 1024, 1024, 32, 16
M = K * N


def _quantile_huber_slope(d, tau):
    below = np.where(d < 0.0, 1.0, 0.0)
    weight = np.abs(tau[None, None, :, None] - below)
    return weight * np.minimum(np.maximum(d, -1.0), 1.0)


def draw0():
    s, s2 = mx_kscale(D), mx_kscale(D)
    u = mx_kscale(B)
    common = np.random.standard_normal((D, K, 1))
    spread = np.random.standard_normal((D, K, N))
    wt = (1.1 * common + 0.5 * spread).reshape(D, M) / np.sqrt(D)
    h = bf(np.random.standard_normal((B, D)) * s)
    hn = bf(np.random.standard_normal((B, D)) * s2)
    w_words, w_scales = pack_weight(np.random.standard_normal((D, M)) * 0.7 / np.sqrt(D) / s[:, None], "e4m3")
    wt_words, wt_scales = pack_weight(wt / s2[:, None], "e4m3")
    return {
        "h": h,
        "hn": hn,
        "w_words": w_words,
        "w_scales": w_scales,
        "wt_words": wt_words,
        "wt_scales": wt_scales,
        "r": bf(np.random.standard_normal(B) * 0.5),
        "a": bf(np.random.uniform(0.5, 1.5, B) * u),
        "c": bf((1.0 + 0.1 * np.random.standard_normal(B)) / u),
    }


def core(h, hn, w_words, w_scales, wt_words, wt_scales, r, a, c):
    h, hn, r, a, c = f64(h), f64(hn), f64(r), f64(a), f64(c)
    w = unpack_weight(w_words, w_scales, "e4m3")
    wt = unpack_weight(wt_words, wt_scales, "e4m3")
    batch = h.shape[0]
    cols = w.shape[1]

    theta = (mxq(h, 1, "e4m3") @ w).reshape(batch, K, N)

    y = (r[:, None] + 0.97 * (mxq(hn, 1, "e4m3") @ wt)).reshape(batch, K, N)

    d = y[:, :, None, :] - theta[:, :, :, None]
    tau = (np.arange(N) + 0.5) / N

    e = -(batch ** -0.5) * np.mean(_quantile_huber_slope(d, tau), axis=-1)
    e = e.reshape(batch, cols)

    return mxq(h * a[:, None], 0, "e4m3").T @ mxq(e * c[:, None], 0, "e4m3")


def setup_inputs():
    drawn = draw0()
    full = np.asarray(drawn['hn']).astype(np.float64)
    scale = (np.abs(full).reshape(1024, 8, 128).max(axis=(2,)) / 448.0).astype(np.float32)
    given = {}
    for key, value in drawn.items():
        if key == 'hn':
            given['hn_bytes'] = e4m3fn_bytes(full / np.repeat(scale.astype(np.float64), 128, axis=1))
            given['hn_scale'] = scale
        else:
            given[key] = value
    return given


def reference(h, hn_bytes, hn_scale, w_words, w_scales, wt_words, wt_scales, r, a, c):
    return core(h, e4m3fn_values(hn_bytes) * np.repeat(hn_scale.astype(np.float64), 128, axis=1), w_words, w_scales, wt_words, wt_scales, r, a, c)

@@ -1,0 +1,380 @@
+from contextlib import ExitStack
+
+import concourse.mybir as mybir
+from concourse.masks import make_identity
+
+F32 = mybir.dt.float32
+BF16 = mybir.dt.bfloat16
+I32 = mybir.dt.int32
+U32 = mybir.dt.uint32
+U8 = mybir.dt.uint8
+FP8 = mybir.dt.float8_e4m3fn
+FP8X4 = mybir.dt.float8_e4m3fn_x4
+ALU = mybir.AluOpType
+ACT = mybir.ActivationFunctionType
+
+P = 128
+B, D, K, N = 1024, 1024, 32, 16
+M = K * N
+FLOPS = 3 * 2 * B * D * M
+G = 2
+TILES = 8
+GAMMA = 0.97
+LIM = 1.0 / GAMMA
+
+
+def tile_ensemblequantilehuberheadweightgrad_d1p_kernel(
+    tc, h, hn_bytes, hn_scale, w_words, w_scales, wt_words, wt_scales, r, a, c, out
+):
+    nc = tc.nc
+    with ExitStack() as ctx:
+        ctx.enter_context(nc.allow_non_contiguous_dma(reason="small per-row vectors"))
+        keep = ctx.enter_context(tc.tile_pool(name="keep", bufs=1))
+        work = ctx.enter_context(tc.tile_pool(name="work", bufs=2))
+        units = ctx.enter_context(tc.tile_pool(name="units", bufs=4))
+        psum = ctx.enter_context(tc.psum_pool(name="psum", bufs=2))
+        ctx.enter_context(tc.manual_schedule())
+
+        w_sc = keep.tile([P, M], U8, name="w_sc", align_bytes=64)
+        wt_sc = keep.tile([P, M], U8, name="wt_sc", align_bytes=64)
+        nc.vector.memset(wt_sc[:].bitcast(I32), 0)
+        nc.vector.memset(w_sc[:].bitcast(I32), 0)
+        dummy = keep.tile([P, 1], F32, name="dummy")
+        nc.vector.memset(dummy[:], 0.0)
+        dummy2 = keep.tile([P, 1], F32, name="dummy2")
+        nc.scalar.activation(out=dummy2[:], in_=dummy[:], func=ACT.Relu)
+        ident = keep.tile([P, P], F32, name="ident", align_bytes=64)
+        make_identity(nc, ident[:])
+        iota_t = keep.tile([P, 1], I32, name="iota_t")
+        nc.gpsimd.iota(out=iota_t[:], pattern=[[0, 1]], base=0, channel_multiplier=1)
+
+        for q in range(4):
+            nc.scalar.dma_start(out=wt_sc[32 * q : 32 * q + 8, :].bitcast(I32), in_=wt_scales[:, 4 * q : 4 * q + 4, :].bitcast(I32))
+        for q in range(4):
+            nc.scalar.dma_start(out=w_sc[32 * q : 32 * q + 8, :].bitcast(I32), in_=w_scales[:, 4 * q : 4 * q + 4, :].bitcast(I32))
+
+        hv = h.rearrange("(g p t) f -> g t p f", p=P, t=4)
+        hnv = hn_bytes.rearrange("(g p t) f -> g t p f", p=P, t=4)
+        h_raw = [keep.tile([P, 4, D], BF16, name="h_raw%d" % g, align_bytes=64) for g in range(G)]
+        hn_raw = [keep.tile([P, D], U8, name="hn_raw%d" % n, align_bytes=64) for n in range(TILES)]
+        hn_sc = keep.tile([P, G, 4, 8], F32, name="hn_sc")
+        w_sb = keep.tile([P, G, M], U32, name="w_sb", align_bytes=64)
+        wt_sb = keep.tile([P, G, M], U32, name="wt_sb", align_bytes=64)
+        r_bf = keep.tile([P, G, 4], BF16, name="r_bf")
+        a_bf = keep.tile([P, G, 4], BF16, name="a_bf")
+        c_bf = keep.tile([P, G, 4], BF16, name="c_bf")
+
+        def load_tile(n):
+            nc.sync.dma_start(out=hn_raw[n][:], in_=hnv[n // 4, n % 4])
+            nc.sync.dma_start(out=h_raw[n // 4][:, n % 4, :], in_=hv[n // 4, n % 4])
+
+        nc.sync.dma_start(out=hn_sc[:], in_=hn_scale.rearrange("(g p t) q -> p g t q", p=P, t=4))
+        load_tile(0)
+        for g in range(G):
+            nc.sync.dma_start(out=wt_sb[:, g, :].bitcast(I32), in_=wt_words[g].rearrange("p n t -> p (n t)").bitcast(I32))
+        for g in range(G):
+            nc.sync.dma_start(out=w_sb[:, g, :].bitcast(I32), in_=w_words[g].rearrange("p n t -> p (n t)").bitcast(I32))
+        nc.sync.dma_start(out=r_bf[:], in_=r.rearrange("(g p t) -> p g t", p=P, t=4))
+        load_tile(1)
+        nc.sync.dma_start(out=a_bf[:], in_=a.rearrange("(g p t) -> p g t", p=P, t=4))
+        nc.sync.dma_start(out=c_bf[:], in_=c.rearrange("(g p t) -> p g t", p=P, t=4))
+        for n in range(2, TILES):
+            load_tile(n)
+
+        i_int = keep.tile([P, 1], I32, name="i_int")
+        nc.vector.tensor_scalar(out=i_int[:], in0=iota_t[:], scalar1=15, scalar2=None, op0=ALU.bitwise_and)
+        i_f = keep.tile([P, 1], F32, name="i_f")
+        nc.vector.tensor_copy(out=i_f[:], in_=i_int[:])
+        alpha = keep.tile([P, 1], F32, name="alpha")
+        nc.vector.tensor_scalar(out=alpha[:], in0=i_f[:], scalar1=2.0 * GAMMA / 16384.0, scalar2=-31.0 * GAMMA / 16384.0, op0=ALU.mult, op1=ALU.add)
+        beta = keep.tile([P, 1], F32, name="beta")
+        nc.vector.tensor_scalar(out=beta[:], in0=i_f[:], scalar1=-2.0 * GAMMA / 8192.0, scalar2=15.0 * GAMMA / 8192.0, op0=ALU.mult, op1=ALU.add)
+        neg_r = keep.tile([P, G * 4], F32, name="neg_r")
+        a_f = keep.tile([P, G * 4], F32, name="a_f")
+        c_f = keep.tile([P, G * 4], F32, name="c_f")
+
+        hn_bf = {}
+        codes = {}
+        cscal = {}
+        grp = {}
+        tr_ps = {}
+        th = {}
+        y_ps = {}
+
+        def widen(n, eng):
+            t = work.tile([P, D], BF16, name="hn_bf", bufs=3, align_bytes=64)
+            hn_bf[n] = t
+            for q in range(8):
+                cols = slice(128 * q, 128 * q + 128)
+                src = hn_raw[n][:, cols].bitcast(FP8)
+                scale = hn_sc[:, n // 4, n % 4, q : q + 1]
+                if eng == "v":
+                    nc.vector.tensor_scalar(out=t[:, cols], in0=src, scalar1=scale, scalar2=None, op0=ALU.mult)
+                else:
+                    nc.scalar.activation(out=t[:, cols], in_=src, func=ACT.Copy, scale=scale)
+
+        def transposes(n, which):
+            if which == 0:
+                words = h_raw[n // 4][:, n % 4, :].bitcast(F32)
+            else:
+                words = hn_bf[n][:].bitcast(F32)
+            wk = psum.tile([P, 4, P], F32, name="wk")
+            tr_ps[n, which] = wk
+            for s in range(2):
+                for u in range(2):
+                    nc.tensor.transpose(wk[:, 2 * s + u, :], words[:, 256 * s + u : 256 * (s + 1) : 2], ident[:])
+
+        def evac(n, which, eng):
+            if n not in grp:
+                gt_ = work.tile([P, 2, 2, P, 2], F32, name="grp", bufs=3, align_bytes=64)
+                grp[n] = gt_
+            dst = grp[n][:, which]
+            src = tr_ps[n, which][:].rearrange("p (s u) r -> p s r u", u=2)
+            if eng == "v":
+                nc.vector.tensor_copy(out=dst, in_=src)
+            else:
+                nc.scalar.copy(out=dst, in_=src)
+
+        def quant(n):
+            cd = work.tile([P, 2, 2, P], U32, name="codes", bufs=3, align_bytes=64)
+            cs = work.tile([P, 2, 2, P], U8, name="cscal", bufs=3, align_bytes=64)
+            codes[n], cscal[n] = cd, cs
+            nc.vector.quantize_mx(
+                out=cd[:].rearrange("p w s r -> p (w s r)").bitcast(FP8X4),
+                scales=cs[:].rearrange("p w s r -> p (w s r)"),
+                in_=grp[n][:].rearrange("p w s r u -> p (w s r u)").bitcast(BF16),
+            )
+
+        def mm(n, which):
+            if which == 0:
+                o = psum.tile([P, M], F32, name="wk")
+                words, sc = w_sb, w_sc
+                tr_ps[n, "th"] = o
+            else:
+                o = psum.tile([P, M], F32, name="y")
+                words, sc = wt_sb, wt_sc
+                y_ps[n] = o
+            for s in range(2):
+                nc.tensor.matmul_mx(
+                    out=o[:],
+                    lhsT=codes[n][:, which, s, :].bitcast(FP8X4),
+                    lhsT_scale=cscal[n][:, which, s, :],
+                    rhs=words[:, s, :].bitcast(FP8X4),
+                    rhs_scale=sc[4 * s : P, :],
+                    start=(s == 0),
+                    stop=(s == 1),
+                )
+
+        def ev_theta(n):
+            t = work.tile([P, M], F32, name="th", bufs=3, align_bytes=64)
+            th[n] = t
+            nc.scalar.activation(out=t[:], in_=tr_ps[n, "th"][:], func=ACT.Identity, bias=neg_r[:, n : n + 1], scale=LIM)
+
+        dd = {}
+        pp = {}
+        sc_ps = {}
+        sp_ps = {}
+
+        def stage_a(u):
+            n, cb = u // 4, u % 4
+            t = units.tile([P, 16, P], F32, name="dd", bufs=5, align_bytes=64)
+            dd[u] = t
+            cols = slice(P * cb, P * cb + P)
+            yv = y_ps[n][:, cols].rearrange("p (k j) -> p j k", j=16).unsqueeze(3).to_broadcast([P, 16, 8, 16])
+            tv = th[n][:, cols].rearrange("p (k i) -> p k i", i=16).unsqueeze(1).to_broadcast([P, 16, 8, 16])
+            nc.vector.tensor_tensor(out=t[:].rearrange("p j (k i) -> p j k i", i=16), in0=yv, in1=tv, op=ALU.subtract)
+
+        def stage_b(u):
+            nc.gpsimd.tensor_scalar(out=dd[u][:], in0=dd[u][:], scalar1=-LIM, scalar2=LIM, op0=ALU.max, op1=ALU.min)
+
+        def stage_d(u):
+            t = units.tile([P, 16, P], F32, name="pp", bufs=4, align_bytes=64)
+            pp[u] = t
+            nc.scalar.activation(out=t[:], in_=dd[u][:], func=ACT.Relu)
+
+        def sums(u, src, store, nm):
+            n, cb = u // 4, u % 4
+            if cb == 0:
+                o = psum.tile([P, M], F32, name=nm)
+                store[n] = o
+            for j in range(16):
+                nc.tensor.matmul(
+                    out=store[n][:, P * cb : P * cb + P],
+                    lhsT=src[u][:, j, :],
+                    rhs=ident[:],
+                    start=(j == 0),
+                    stop=(j == 15),
+                    is_transpose=True,
+                )
+
+        t1 = {}
+        gt = {}
+        gb = {}
+        ec = {}
+
+        def post1(n):
+            t = work.tile([P, M], F32, name="t1", align_bytes=64)
+            t1[n] = t
+            nc.scalar.activation(out=t[:], in_=sp_ps[n][:], func=ACT.Copy, scale=beta[:, 0:1])
+
+        def post2(n):
+            t = work.tile([P, M], F32, name="gt", align_bytes=64)
+            gt[n] = t
+            nc.vector.scalar_tensor_tensor(out=t[:], in0=sc_ps[n][:], scalar=alpha[:, 0:1], in1=t1[n][:], op0=ALU.mult, op1=ALU.add)
+
+        def post3(n):
+            wk = psum.tile([P, M], F32, name="wk")
+            gb[n] = wk
+            for cb in range(4):
+                cols = slice(P * cb, P * cb + P)
+                nc.tensor.transpose(wk[:, cols], gt[n][:, cols], ident[:])
+
+        def post4(n):
+            g, t = n // 4, n % 4
+            if t == 0:
+                e_ = work.tile([P, 4, M], BF16, name="ec", bufs=1, align_bytes=64)
+                ec[g] = e_
+            nc.scalar.activation(out=ec[g][:, t, :], in_=gb[n][:], func=ACT.Copy, scale=c_f[:, n : n + 1])
+
+        eq_codes = {}
+        eq_scal = {}
+        ha = {}
+        ha_codes = {}
+        ha_scal = {}
+
+        def e_interleave(g):
+            t = work.tile([P, M, 4], BF16, name="ecg", bufs=1, align_bytes=64)
+            eq_codes[g, "in"] = t
+            nc.vector.tensor_copy(out=t[:], in_=ec[g][:].rearrange("p t m -> p m t"))
+
+        def e_quant(g):
+            cd = keep.tile([P, M], U32, name="eq_codes%d" % g, align_bytes=64)
+            cs = keep.tile([P, M], U8, name="eq_scal%d" % g, align_bytes=64)
+            eq_codes[g], eq_scal[g] = cd, cs
+            nc.vector.quantize_mx(out=cd[:].bitcast(FP8X4), scales=cs[:], in_=eq_codes[g, "in"][:].rearrange("p m t -> p (m t)"))
+
+        def ha_chunk(g, x):
+            if x == 0:
+                t = keep.tile([P, D, 4], BF16, name="ha%d" % g, align_bytes=64)
+                ha[g] = t
+            f = slice(256 * x, 256 * x + 256)
+            nc.gpsimd.tensor_tensor(
+                out=ha[g][:, f, :],
+                in0=h_raw[g][:, :, f].rearrange("p t f -> p f t"),
+                in1=a_f[:, 4 * g : 4 * g + 4].unsqueeze(1).to_broadcast([P, 256, 4]),
+                op=ALU.mult,
+            )
+
+        def ha_quant(g):
+            cd = keep.tile([P, D], U32, name="ha_codes%d" % g, align_bytes=64)
+            cs = keep.tile([P, D], U8, name="ha_scal%d" % g, align_bytes=64)
+            ha_codes[g], ha_scal[g] = cd, cs
+            nc.vector.quantize_mx(out=cd[:].bitcast(FP8X4), scales=cs[:], in_=ha[g][:].rearrange("p f t -> p (f t)"))
+
+        dw = {}
+
+        def dw_pass(m, tag, g):
+            if g == 0:
+                o = psum.tile([P, M], F32, name=tag)
+                dw[m] = o
+            cols = slice(P * m, P * m + P)
+            nc.tensor.matmul_mx(
+                out=dw[m][:],
+                lhsT=ha_codes[g][:, cols].bitcast(FP8X4),
+                lhsT_scale=ha_scal[g][:, cols],
+                rhs=eq_codes[g][:].bitcast(FP8X4),
+                rhs_scale=eq_scal[g][:],
+                start=(g == 0),
+                stop=(g == G - 1),
+            )
+
+        def dw_out(m):
+            t = work.tile([P, M], F32, name="res", bufs=4, align_bytes=64)
+            if m % 2 == 0:
+                nc.vector.tensor_copy(out=t[:], in_=dw[m][:])
+            else:
+                nc.scalar.copy(out=t[:], in_=dw[m][:])
+            nc.sync.dma_start(out=out[P * m : P * m + P, :], in_=t[:])
+
+        widen(0, "v")
+        transposes(0, 0)
+        evac(0, 0, "s")
+        transposes(0, 1)
+        evac(0, 1, "v")
+        quant(0)
+        nc.vector.tensor_scalar(out=neg_r[:], in0=r_bf[:].rearrange("p g t -> p (g t)"), scalar1=-LIM, scalar2=None, op0=ALU.mult)
+        mm(0, 0)
+        mm(0, 1)
+        ev_theta(0)
+        widen(1, "s")
+        nc.scalar.copy(out=a_f[:], in_=a_bf[:].rearrange("p g t -> p (g t)"))
+        nc.scalar.copy(out=c_f[:], in_=c_bf[:].rearrange("p g t -> p (g t)"))
+
+        n_units = 4 * TILES
+        for s in range(n_units + 4):
+            n, ph = s // 4, s % 4
+            if s < n_units:
+                stage_a(s)
+            if s == 0:
+                transposes(1, 0)
+                transposes(1, 1)
+                evac(1, 0, "v")
+                evac(1, 1, "s")
+                quant(1)
+                widen(2, "s")
+            if ph == 1 and n + 2 < TILES:
+                quant(n + 2)
+            if s == 11:
+                ha_quant(0)
+            if s == 27:
+                ha_quant(1)
+            if 1 <= s <= n_units:
+                stage_b(s - 1)
+            if s in (1, 3, 5, 7):
+                ha_chunk(0, s // 2)
+            if s in (17, 19, 21, 23):
+                ha_chunk(1, (s - 17) // 2)
+            if 2 <= s <= n_units + 1:
+                stage_d(s - 2)
+                sums(s - 2, dd, sc_ps, "sc")
+            if 3 <= s <= n_units + 2:
+                sums(s - 3, pp, sp_ps, "sp")
+            if ph == 0 and n + 2 < TILES:
+                transposes(n + 2, 0)
+                transposes(n + 2, 1)
+                evac(n + 2, 0, "v")
+                evac(n + 2, 1, "s")
+            if ph == 1 and n + 3 < TILES:
+                widen(n + 3, "s")
+            if ph == 2 and n + 1 < TILES:
+                mm(n + 1, 0)
+                mm(n + 1, 1)
+                ev_theta(n + 1)
+            if ph == 3 and 1 <= n <= TILES - 1:
+                post1(n - 1)
+            if ph == 0 and 2 <= n <= TILES:
+                post2(n - 2)
+            if ph == 1 and 2 <= n <= TILES:
+                post3(n - 2)
+                post4(n - 2)
+            if s == 22:
+                e_interleave(0)
+            if s == 23:
+                e_quant(0)
+
+        order = ["y", "y", "sc", "sp", "sc", "sp", "wk", "wk"]
+        for m in range(4):
+            dw_pass(m, order[m], 0)
+        post1(TILES - 1)
+        post2(TILES - 1)
+        post3(TILES - 1)
+        post4(TILES - 1)
+        e_interleave(1)
+        e_quant(1)
+        for m in range(4):
+            dw_pass(m, order[m], 1)
+            dw_out(m)
+        for m in range(4, 8):
+            dw_pass(m, order[m], 0)
+            dw_pass(m, order[m], 1)
+            dw_out(m)

@@ -19,6 +19,7 @@ M = K * N
 FLOPS = 3 * 2 * B * D * M
 G = 2
 TILES = 8
+SEQ = [(n, cb) for n in range(6) for cb in range(4)] + [(6, 0), (6, 1), (7, 0), (7, 1), (6, 2), (7, 2), (6, 3), (7, 3)]
 GAMMA = 0.97
 LIM = 1.0 / GAMMA
 
@@ -42,16 +43,10 @@ def tile_ensemblequantilehuberheadweightgrad_d1p_kernel(
         dummy = keep.tile([P, 1], F32, name="dummy")
         nc.vector.memset(dummy[:], 0.0)
         dummy2 = keep.tile([P, 1], F32, name="dummy2")
-        nc.scalar.activation(out=dummy2[:], in_=dummy[:], func=ACT.Relu)
         ident = keep.tile([P, P], F32, name="ident", align_bytes=64)
         make_identity(nc, ident[:])
         iota_t = keep.tile([P, 1], I32, name="iota_t")
         nc.gpsimd.iota(out=iota_t[:], pattern=[[0, 1]], base=0, channel_multiplier=1)
-
-        for q in range(4):
-            nc.scalar.dma_start(out=wt_sc[32 * q : 32 * q + 8, :].bitcast(I32), in_=wt_scales[:, 4 * q : 4 * q + 4, :].bitcast(I32))
-        for q in range(4):
-            nc.scalar.dma_start(out=w_sc[32 * q : 32 * q + 8, :].bitcast(I32), in_=w_scales[:, 4 * q : 4 * q + 4, :].bitcast(I32))
 
         hv = h.rearrange("(g p t) f -> g t p f", p=P, t=4)
         hnv = hn_bytes.rearrange("(g p t) f -> g t p f", p=P, t=4)
@@ -68,12 +63,14 @@ def tile_ensemblequantilehuberheadweightgrad_d1p_kernel(
             nc.sync.dma_start(out=hn_raw[n][:], in_=hnv[n // 4, n % 4])
             nc.sync.dma_start(out=h_raw[n // 4][:, n % 4, :], in_=hv[n // 4, n % 4])
 
+        nc.scalar.activation(out=dummy2[:], in_=dummy[:], func=ACT.Relu)
         nc.sync.dma_start(out=hn_sc[:], in_=hn_scale.rearrange("(g p t) q -> p g t q", p=P, t=4))
         load_tile(0)
-        for g in range(G):
-            nc.sync.dma_start(out=wt_sb[:, g, :].bitcast(I32), in_=wt_words[g].rearrange("p n t -> p (n t)").bitcast(I32))
-        for g in range(G):
-            nc.sync.dma_start(out=w_sb[:, g, :].bitcast(I32), in_=w_words[g].rearrange("p n t -> p (n t)").bitcast(I32))
+        for words, scal, w_in, s_in in ((w_sb, w_sc, w_words, w_scales), (wt_sb, wt_sc, wt_words, wt_scales)):
+            for g in range(G):
+                nc.sync.dma_start(out=words[:, g, :].bitcast(I32), in_=w_in[g].rearrange("p n t -> p (n t)").bitcast(I32))
+            for q in range(4):
+                nc.sync.dma_start(out=scal[32 * q : 32 * q + 8, :].bitcast(I32), in_=s_in[:, 4 * q : 4 * q + 4, :].bitcast(I32))
         nc.sync.dma_start(out=r_bf[:], in_=r.rearrange("(g p t) -> p g t", p=P, t=4))
         load_tile(1)
         nc.sync.dma_start(out=a_bf[:], in_=a.rearrange("(g p t) -> p g t", p=P, t=4))
@@ -82,13 +79,9 @@ def tile_ensemblequantilehuberheadweightgrad_d1p_kernel(
             load_tile(n)
 
         i_int = keep.tile([P, 1], I32, name="i_int")
-        nc.vector.tensor_scalar(out=i_int[:], in0=iota_t[:], scalar1=15, scalar2=None, op0=ALU.bitwise_and)
         i_f = keep.tile([P, 1], F32, name="i_f")
-        nc.vector.tensor_copy(out=i_f[:], in_=i_int[:])
         alpha = keep.tile([P, 1], F32, name="alpha")
-        nc.vector.tensor_scalar(out=alpha[:], in0=i_f[:], scalar1=2.0 * GAMMA / 16384.0, scalar2=-31.0 * GAMMA / 16384.0, op0=ALU.mult, op1=ALU.add)
         beta = keep.tile([P, 1], F32, name="beta")
-        nc.vector.tensor_scalar(out=beta[:], in0=i_f[:], scalar1=-2.0 * GAMMA / 8192.0, scalar2=15.0 * GAMMA / 8192.0, op0=ALU.mult, op1=ALU.add)
         neg_r = keep.tile([P, G * 4], F32, name="neg_r")
         a_f = keep.tile([P, G * 4], F32, name="a_f")
         c_f = keep.tile([P, G * 4], F32, name="c_f")
@@ -101,17 +94,18 @@ def tile_ensemblequantilehuberheadweightgrad_d1p_kernel(
         th = {}
         y_ps = {}
 
-        def widen(n, eng):
-            t = work.tile([P, D], BF16, name="hn_bf", bufs=3, align_bytes=64)
-            hn_bf[n] = t
-            for q in range(8):
+        def widen(n, eng, blocks):
+            if n not in hn_bf:
+                t = work.tile([P, D], BF16, name="hn_bf", bufs=3, align_bytes=64)
+                hn_bf[n] = t
+            for q in blocks:
                 cols = slice(128 * q, 128 * q + 128)
                 src = hn_raw[n][:, cols].bitcast(FP8)
                 scale = hn_sc[:, n // 4, n % 4, q : q + 1]
                 if eng == "v":
-                    nc.vector.tensor_scalar(out=t[:, cols], in0=src, scalar1=scale, scalar2=None, op0=ALU.mult)
+                    nc.vector.tensor_scalar(out=hn_bf[n][:, cols], in0=src, scalar1=scale, scalar2=None, op0=ALU.mult)
                 else:
-                    nc.scalar.activation(out=t[:, cols], in_=src, func=ACT.Copy, scale=scale)
+                    nc.scalar.activation(out=hn_bf[n][:, cols], in_=src, func=ACT.Copy, scale=scale)
 
         def transposes(n, which):
             if which == 0:
@@ -135,14 +129,16 @@ def tile_ensemblequantilehuberheadweightgrad_d1p_kernel(
             else:
                 nc.scalar.copy(out=dst, in_=src)
 
-        def quant(n):
-            cd = work.tile([P, 2, 2, P], U32, name="codes", bufs=3, align_bytes=64)
-            cs = work.tile([P, 2, 2, P], U8, name="cscal", bufs=3, align_bytes=64)
-            codes[n], cscal[n] = cd, cs
+        def quant(n, parts):
+            if n not in codes:
+                cd = work.tile([P, 2, 2 * P], U32, name="codes", bufs=3, align_bytes=64)
+                cs = work.tile([P, 2, 2 * P], U8, name="cscal", bufs=3, align_bytes=64)
+                codes[n], cscal[n] = cd, cs
+            cd, cs = codes[n], cscal[n]
             nc.vector.quantize_mx(
-                out=cd[:].rearrange("p w s r -> p (w s r)").bitcast(FP8X4),
-                scales=cs[:].rearrange("p w s r -> p (w s r)"),
-                in_=grp[n][:].rearrange("p w s r u -> p (w s r u)").bitcast(BF16),
+                out=cd[:, parts, :].rearrange("p w r -> p (w r)").bitcast(FP8X4),
+                scales=cs[:, parts, :].rearrange("p w r -> p (w r)"),
+                in_=grp[n][:, parts].rearrange("p w s r u -> p (w s r u)").bitcast(BF16),
             )
 
         def mm(n, which):
@@ -157,8 +153,8 @@ def tile_ensemblequantilehuberheadweightgrad_d1p_kernel(
             for s in range(2):
                 nc.tensor.matmul_mx(
                     out=o[:],
-                    lhsT=codes[n][:, which, s, :].bitcast(FP8X4),
-                    lhsT_scale=cscal[n][:, which, s, :],
+                    lhsT=codes[n][:, which, P * s : P * s + P].bitcast(FP8X4),
+                    lhsT_scale=cscal[n][:, which, P * s : P * s + P],
                     rhs=words[:, s, :].bitcast(FP8X4),
                     rhs_scale=sc[4 * s : P, :],
                     start=(s == 0),
@@ -175,206 +171,256 @@ def tile_ensemblequantilehuberheadweightgrad_d1p_kernel(
         sc_ps = {}
         sp_ps = {}
 
-        def stage_a(u):
-            n, cb = u // 4, u % 4
-            t = units.tile([P, 16, P], F32, name="dd", bufs=5, align_bytes=64)
-            dd[u] = t
+        def stage_a(u, j0=0, j1=16):
+            n, cb = SEQ[u]
+            if j0 == 0:
+                t = units.tile([P, 16, P], F32, name="dd", bufs=5, align_bytes=64)
+                dd[u] = t
             cols = slice(P * cb, P * cb + P)
-            yv = y_ps[n][:, cols].rearrange("p (k j) -> p j k", j=16).unsqueeze(3).to_broadcast([P, 16, 8, 16])
-            tv = th[n][:, cols].rearrange("p (k i) -> p k i", i=16).unsqueeze(1).to_broadcast([P, 16, 8, 16])
-            nc.vector.tensor_tensor(out=t[:].rearrange("p j (k i) -> p j k i", i=16), in0=yv, in1=tv, op=ALU.subtract)
+            yv = y_ps[n][:, cols].rearrange("p (k j) -> p j k", j=16)[:, j0:j1, :].unsqueeze(3).to_broadcast([P, j1 - j0, 8, 16])
+            tv = th[n][:, cols].rearrange("p (k i) -> p k i", i=16).unsqueeze(1).to_broadcast([P, j1 - j0, 8, 16])
+            nc.vector.tensor_tensor(out=dd[u][:, j0:j1, :].rearrange("p j (k i) -> p j k i", i=16), in0=yv, in1=tv, op=ALU.subtract)
 
-        def stage_b(u):
-            nc.gpsimd.tensor_scalar(out=dd[u][:], in0=dd[u][:], scalar1=-LIM, scalar2=LIM, op0=ALU.max, op1=ALU.min)
+        def stage_b(u, j0=0, j1=16):
+            nc.vector.tensor_scalar(out=dd[u][:, j0:j1, :], in0=dd[u][:, j0:j1, :], scalar1=-LIM, scalar2=LIM, op0=ALU.max, op1=ALU.min)
 
-        def stage_d(u):
-            t = units.tile([P, 16, P], F32, name="pp", bufs=4, align_bytes=64)
-            pp[u] = t
-            nc.scalar.activation(out=t[:], in_=dd[u][:], func=ACT.Relu)
+        def stage_d(u, eng="s", j0=0, j1=16):
+            if j0 == 0:
+                t = units.tile([P, 16, P], F32, name="pp", bufs=4, align_bytes=64)
+                pp[u] = t
+            dst, src = pp[u][:, j0:j1, :], dd[u][:, j0:j1, :]
+            if eng == "s":
+                nc.scalar.activation(out=dst, in_=src, func=ACT.Relu)
+            else:
+                nc.vector.tensor_scalar(out=dst, in0=src, scalar1=0.0, scalar2=None, op0=ALU.max)
 
-        def sums(u, src, store, nm):
-            n, cb = u // 4, u % 4
-            if cb == 0:
-                o = psum.tile([P, M], F32, name=nm)
-                store[n] = o
-            for j in range(16):
-                nc.tensor.matmul(
-                    out=store[n][:, P * cb : P * cb + P],
-                    lhsT=src[u][:, j, :],
-                    rhs=ident[:],
-                    start=(j == 0),
-                    stop=(j == 15),
-                    is_transpose=True,
-                )
+        def sums(u, src, store, nm, j0=0, j1=16):
+            n, cb = SEQ[u]
+            key = n if n < 6 else ("pair", cb)
+            x = cb if n < 6 else n - 6
+            if x == 0 and j0 == 0:
+                o = psum.tile([P, M if n < 6 else 2 * P], F32, name=nm)
+                store[key] = o
+            dst = store[key][:, P * x : P * x + P]
+            for j in range(j0, j1):
+                nc.tensor.matmul(out=dst, lhsT=src[u][:, j, :], rhs=ident[:], start=(j == 0), stop=(j == 15), is_transpose=True)
 
-        t1 = {}
-        gt = {}
+        gs = {}
         gb = {}
         ec = {}
 
-        def post1(n):
-            t = work.tile([P, M], F32, name="t1", align_bytes=64)
-            t1[n] = t
-            nc.scalar.activation(out=t[:], in_=sp_ps[n][:], func=ACT.Copy, scale=beta[:, 0:1])
+        def post1(key, width, which):
+            store, fac = (sc_ps, alpha) if which == 0 else (sp_ps, beta)
+            t = work.tile([P, width], F32, name="gs%d" % which, align_bytes=64)
+            gs[key, which] = t
+            nc.scalar.activation(out=t[:], in_=store[key][:], func=ACT.Copy, scale=fac[:, 0:1])
 
-        def post2(n):
-            t = work.tile([P, M], F32, name="gt", align_bytes=64)
-            gt[n] = t
-            nc.vector.scalar_tensor_tensor(out=t[:], in0=sc_ps[n][:], scalar=alpha[:, 0:1], in1=t1[n][:], op0=ALU.mult, op1=ALU.add)
+        def post3(key, width):
+            wk = psum.tile([P, width], F32, name="wk")
+            gb[key] = wk
+            for x in range(width // P):
+                cols = slice(P * x, P * x + P)
+                for which in range(2):
+                    nc.tensor.matmul(out=wk[:, cols], lhsT=gs[key, which][:, cols], rhs=ident[:], start=(which == 0), stop=(which == 1), is_transpose=True)
 
-        def post3(n):
-            wk = psum.tile([P, M], F32, name="wk")
-            gb[n] = wk
-            for cb in range(4):
-                cols = slice(P * cb, P * cb + P)
-                nc.tensor.transpose(wk[:, cols], gt[n][:, cols], ident[:])
-
-        def post4(n):
+        def post4(key, n, cols, src):
             g, t = n // 4, n % 4
-            if t == 0:
-                e_ = work.tile([P, 4, M], BF16, name="ec", bufs=1, align_bytes=64)
+            if g not in ec:
+                e_ = work.tile([P, 4, M], BF16, name="ec", align_bytes=64)
                 ec[g] = e_
-            nc.scalar.activation(out=ec[g][:, t, :], in_=gb[n][:], func=ACT.Copy, scale=c_f[:, n : n + 1])
+            nc.scalar.activation(out=ec[g][:, t, cols], in_=gb[key][:, src], func=ACT.Copy, scale=c_f[:, n : n + 1])
 
-        eq_codes = {}
-        eq_scal = {}
+        e_in = {}
+        e_codes = {}
+        e_scal = {}
         ha = {}
         ha_codes = {}
         ha_scal = {}
 
-        def e_interleave(g):
-            t = work.tile([P, M, 4], BF16, name="ecg", bufs=1, align_bytes=64)
-            eq_codes[g, "in"] = t
-            nc.vector.tensor_copy(out=t[:], in_=ec[g][:].rearrange("p t m -> p m t"))
+        def e_interleave(g, cols, eng):
+            if g not in e_in:
+                t = work.tile([P, M, 4], BF16, name="e_in", align_bytes=64)
+                e_in[g] = t
+            (nc.vector.tensor_copy if eng == "v" else nc.scalar.copy)(out=e_in[g][:, cols, :], in_=ec[g][:, :, cols].rearrange("p t m -> p m t"))
 
-        def e_quant(g):
-            cd = keep.tile([P, M], U32, name="eq_codes%d" % g, align_bytes=64)
-            cs = keep.tile([P, M], U8, name="eq_scal%d" % g, align_bytes=64)
-            eq_codes[g], eq_scal[g] = cd, cs
-            nc.vector.quantize_mx(out=cd[:].bitcast(FP8X4), scales=cs[:], in_=eq_codes[g, "in"][:].rearrange("p m t -> p (m t)"))
+        def e_quant(g, cols):
+            if g not in e_codes:
+                cd = keep.tile([P, M], U32, name="e_codes%d" % g, align_bytes=64)
+                cs = keep.tile([P, M], U8, name="e_scal%d" % g, align_bytes=64)
+                e_codes[g], e_scal[g] = cd, cs
+            nc.vector.quantize_mx(out=e_codes[g][:, cols].bitcast(FP8X4), scales=e_scal[g][:, cols], in_=e_in[g][:, cols, :].rearrange("p m t -> p (m t)"))
 
-        def ha_chunk(g, x):
-            if x == 0:
+        def ha_chunk(x):
+            g, f0 = x // 8, 128 * (x % 8)
+            if x % 8 == 0:
                 t = keep.tile([P, D, 4], BF16, name="ha%d" % g, align_bytes=64)
                 ha[g] = t
-            f = slice(256 * x, 256 * x + 256)
+            f = slice(f0, f0 + 128)
+            ac = work.tile([P, 4], F32, name="ac", bufs=3)
+            nc.vector.tensor_copy(out=ac[:], in_=a_f[:, 4 * g : 4 * g + 4])
             nc.gpsimd.tensor_tensor(
                 out=ha[g][:, f, :],
                 in0=h_raw[g][:, :, f].rearrange("p t f -> p f t"),
-                in1=a_f[:, 4 * g : 4 * g + 4].unsqueeze(1).to_broadcast([P, 256, 4]),
+                in1=ac[:].unsqueeze(1).to_broadcast([P, 128, 4]),
                 op=ALU.mult,
             )
 
-        def ha_quant(g):
-            cd = keep.tile([P, D], U32, name="ha_codes%d" % g, align_bytes=64)
-            cs = keep.tile([P, D], U8, name="ha_scal%d" % g, align_bytes=64)
-            ha_codes[g], ha_scal[g] = cd, cs
-            nc.vector.quantize_mx(out=cd[:].bitcast(FP8X4), scales=cs[:], in_=ha[g][:].rearrange("p f t -> p (f t)"))
+        def ha_quant(g, half):
+            if half == 0:
+                cd = keep.tile([P, D], U32, name="ha_codes%d" % g, align_bytes=64)
+                cs = keep.tile([P, D], U8, name="ha_scal%d" % g, align_bytes=64)
+                ha_codes[g], ha_scal[g] = cd, cs
+            f = slice(512 * half, 512 * half + 512)
+            nc.vector.quantize_mx(out=ha_codes[g][:, f].bitcast(FP8X4), scales=ha_scal[g][:, f], in_=ha[g][:, f, :].rearrange("p f t -> p (f t)"))
 
-        dw = {}
+        out_v = out.rearrange("(m p) c -> p m c", p=P)
 
-        def dw_pass(m, tag, g):
-            if g == 0:
-                o = psum.tile([P, M], F32, name=tag)
-                dw[m] = o
-            cols = slice(P * m, P * m + P)
-            nc.tensor.matmul_mx(
-                out=dw[m][:],
-                lhsT=ha_codes[g][:, cols].bitcast(FP8X4),
-                lhsT_scale=ha_scal[g][:, cols],
-                rhs=eq_codes[g][:].bitcast(FP8X4),
-                rhs_scale=eq_scal[g][:],
-                start=(g == 0),
-                stop=(g == G - 1),
-            )
-
-        def dw_out(m):
-            t = work.tile([P, M], F32, name="res", bufs=4, align_bytes=64)
-            if m % 2 == 0:
-                nc.vector.tensor_copy(out=t[:], in_=dw[m][:])
+        def dw_part(x, part, tag, eng):
+            cols = slice(2 * P * x, 2 * P * x + 2 * P)
+            o = psum.tile([P, 2, 2 * P], F32, name=tag)
+            for y in range(2):
+                f = slice(P * (2 * part + y), P * (2 * part + y) + P)
+                for g in range(G):
+                    nc.tensor.matmul_mx(
+                        out=o[:, y, :],
+                        lhsT=ha_codes[g][:, f].bitcast(FP8X4),
+                        lhsT_scale=ha_scal[g][:, f],
+                        rhs=e_codes[g][:, cols].bitcast(FP8X4),
+                        rhs_scale=e_scal[g][:, cols],
+                        start=(g == 0),
+                        stop=(g == G - 1),
+                    )
+            t = work.tile([P, 2, 2 * P], F32, name="res", bufs=8, align_bytes=64)
+            if eng == "v":
+                nc.vector.tensor_copy(out=t[:], in_=o[:])
             else:
-                nc.scalar.copy(out=t[:], in_=dw[m][:])
-            nc.sync.dma_start(out=out[P * m : P * m + P, :], in_=t[:])
+                nc.scalar.copy(out=t[:], in_=o[:])
+            nc.sync.dma_start(out=out_v[:, 2 * part : 2 * part + 2, cols], in_=t[:])
 
-        widen(0, "v")
+        def e_block(x):
+            e_interleave(1, slice(2 * P * x, 2 * P * x + 2 * P), "v")
+            e_quant(1, slice(2 * P * x, 2 * P * x + 2 * P))
+
+        def pair_post1(cb, which):
+            post1(("pair", cb), 2 * P, which)
+
+        def pair_post3(cb):
+            post3(("pair", cb), 2 * P)
+
+        def pair_post4(cb):
+            cols = slice(P * cb, P * cb + P)
+            post4(("pair", cb), 6, cols, slice(0, P))
+            post4(("pair", cb), 7, cols, slice(P, 2 * P))
+
+        widen(0, "v", range(0, 5))
+        widen(0, "s", range(5, 8))
         transposes(0, 0)
-        evac(0, 0, "s")
+        evac(0, 0, "v")
         transposes(0, 1)
-        evac(0, 1, "v")
-        quant(0)
+        evac(0, 1, "s")
+        quant(0, slice(0, 1))
+        quant(0, slice(1, 2))
         nc.vector.tensor_scalar(out=neg_r[:], in0=r_bf[:].rearrange("p g t -> p (g t)"), scalar1=-LIM, scalar2=None, op0=ALU.mult)
         mm(0, 0)
-        mm(0, 1)
         ev_theta(0)
-        widen(1, "s")
-        nc.scalar.copy(out=a_f[:], in_=a_bf[:].rearrange("p g t -> p (g t)"))
-        nc.scalar.copy(out=c_f[:], in_=c_bf[:].rearrange("p g t -> p (g t)"))
+        mm(0, 1)
+        widen(1, "s", range(8))
 
         n_units = 4 * TILES
-        for s in range(n_units + 4):
+        chunk_slots = [s for s in range(2, 24) if s % 4 != 0][:16]
+        for s in range(n_units):
             n, ph = s // 4, s % 4
-            if s < n_units:
-                stage_a(s)
+            if s in chunk_slots:
+                ha_chunk(chunk_slots.index(s))
+            stage_a(s, 0, 8 if s == n_units - 1 else 16)
             if s == 0:
                 transposes(1, 0)
-                transposes(1, 1)
                 evac(1, 0, "v")
+                transposes(1, 1)
                 evac(1, 1, "s")
-                quant(1)
-                widen(2, "s")
-            if ph == 1 and n + 2 < TILES:
-                quant(n + 2)
-            if s == 11:
-                ha_quant(0)
-            if s == 27:
-                ha_quant(1)
-            if 1 <= s <= n_units:
+                nc.vector.tensor_scalar(out=i_int[:], in0=iota_t[:], scalar1=15, scalar2=None, op0=ALU.bitwise_and)
+                nc.vector.tensor_copy(out=i_f[:], in_=i_int[:])
+                nc.scalar.copy(out=a_f[:], in_=a_bf[:].rearrange("p g t -> p (g t)"))
+                nc.scalar.copy(out=c_f[:], in_=c_bf[:].rearrange("p g t -> p (g t)"))
+                widen(2, "s", range(0, 4))
+            if s == 1:
+                nc.vector.tensor_scalar(out=alpha[:], in0=i_f[:], scalar1=2.0 * GAMMA / 16384.0, scalar2=-31.0 * GAMMA / 16384.0, op0=ALU.mult, op1=ALU.add)
+                nc.vector.tensor_scalar(out=beta[:], in0=i_f[:], scalar1=-2.0 * GAMMA / 8192.0, scalar2=15.0 * GAMMA / 8192.0, op0=ALU.mult, op1=ALU.add)
+            if ph == 0 and n + 1 < TILES:
+                quant(n + 1, slice(0, 2))
+            if s in (15, 18):
+                ha_quant(0, (s - 15) // 3)
+            if s >= 1:
                 stage_b(s - 1)
-            if s in (1, 3, 5, 7):
-                ha_chunk(0, s // 2)
-            if s in (17, 19, 21, 23):
-                ha_chunk(1, (s - 17) // 2)
-            if 2 <= s <= n_units + 1:
-                stage_d(s - 2)
-                sums(s - 2, dd, sc_ps, "sc")
-            if 3 <= s <= n_units + 2:
-                sums(s - 3, pp, sp_ps, "sp")
-            if ph == 0 and n + 2 < TILES:
+                stage_d(s - 1)
+            if ph == 1 and n + 2 < TILES:
                 transposes(n + 2, 0)
+            if ph == 2 and n + 2 < TILES:
                 transposes(n + 2, 1)
-                evac(n + 2, 0, "v")
-                evac(n + 2, 1, "s")
-            if ph == 1 and n + 3 < TILES:
-                widen(n + 3, "s")
-            if ph == 2 and n + 1 < TILES:
+            if s >= 2:
+                sums(s - 2, pp, sp_ps, "sp")
+            if ph == 0 and n + 1 < TILES:
                 mm(n + 1, 0)
                 mm(n + 1, 1)
-                ev_theta(n + 1)
-            if ph == 3 and 1 <= n <= TILES - 1:
-                post1(n - 1)
-            if ph == 0 and 2 <= n <= TILES:
-                post2(n - 2)
-            if ph == 1 and 2 <= n <= TILES:
-                post3(n - 2)
-                post4(n - 2)
+            if ph == 3 and 1 <= n <= TILES - 2:
+                post3(n - 1, M)
+            for u in (26, 27):
+                if s == u + 3:
+                    pair_post3(SEQ[u][1])
+            if s >= 1:
+                sums(s - 1, dd, sc_ps, "sc")
+            if ph == 0:
+                if n + 1 < TILES:
+                    ev_theta(n + 1)
+                if n + 2 < TILES:
+                    widen(n + 2, "s", range(4, 8))
+            if ph == 1:
+                if n + 2 < TILES:
+                    evac(n + 2, 0, "s")
+                if 1 <= n <= TILES - 2:
+                    post1(n - 1, M, 0)
+            if ph == 2:
+                if n + 2 < TILES:
+                    evac(n + 2, 1, "s")
+                if 1 <= n <= TILES - 2:
+                    post1(n - 1, M, 1)
+            if ph == 3:
+                if n + 3 < TILES:
+                    widen(n + 3, "s", range(0, 4))
+                if 1 <= n <= TILES - 2:
+                    post4(n - 1, n - 1, slice(0, M), slice(0, M))
             if s == 22:
-                e_interleave(0)
-            if s == 23:
-                e_quant(0)
+                e_interleave(0, slice(0, M), "s")
+            for u in (26, 27, 29):
+                if s == u + 2:
+                    pair_post1(SEQ[u][1], 0)
+                    pair_post1(SEQ[u][1], 1)
+            for u in (26, 27):
+                if s == u + 3:
+                    pair_post4(SEQ[u][1])
 
-        order = ["y", "y", "sc", "sp", "sc", "sp", "wk", "wk"]
-        for m in range(4):
-            dw_pass(m, order[m], 0)
-        post1(TILES - 1)
-        post2(TILES - 1)
-        post3(TILES - 1)
-        post4(TILES - 1)
-        e_interleave(1)
-        e_quant(1)
-        for m in range(4):
-            dw_pass(m, order[m], 1)
-            dw_out(m)
-        for m in range(4, 8):
-            dw_pass(m, order[m], 0)
-            dw_pass(m, order[m], 1)
-            dw_out(m)
+        stage_b(31, 0, 8)
+        sums(31, dd, sc_ps, "sc", 0, 8)
+        stage_a(31, 8, 16)
+        stage_d(31, "v", 0, 8)
+        stage_b(31, 8, 16)
+        sums(31, dd, sc_ps, "sc", 8, 16)
+        stage_d(31, "v", 8, 16)
+        sums(30, pp, sp_ps, "sp")
+        sums(31, pp, sp_ps, "sp")
+        e_quant(0, slice(0, M))
+        ha_quant(1, 0)
+        ha_quant(1, 1)
+        e_block(0)
+        pair_post1(3, 0)
+        pair_post3(2)
+        pair_post1(3, 1)
+        pair_post4(2)
+        pair_post3(3)
+        pair_post4(3)
+        for part, tag, eng in ((0, "y", "v"), (1, "y", "s"), (2, "sc", "v"), (3, "sp", "s")):
+            dw_part(0, part, tag, eng)
+            if part == 0:
+                e_block(1)
+        for part, tag, eng in ((0, "y", "s"), (1, "y", "v"), (2, "sc", "s"), (3, "sp", "v")):
+            dw_part(1, part, tag, eng)

from contextlib import ExitStack

import concourse.mybir as mybir
from concourse.masks import make_identity

F32 = mybir.dt.float32
BF16 = mybir.dt.bfloat16
I32 = mybir.dt.int32
U32 = mybir.dt.uint32
U8 = mybir.dt.uint8
FP8 = mybir.dt.float8_e4m3fn
FP8X4 = mybir.dt.float8_e4m3fn_x4
ALU = mybir.AluOpType
ACT = mybir.ActivationFunctionType

P = 128
B, D, K, N = 1024, 1024, 32, 16
M = K * N
FLOPS = 3 * 2 * B * D * M
G = 2
TILES = 8
SEQ = [(n, cb) for n in range(6) for cb in range(4)] + [(6, 0), (6, 1), (7, 0), (7, 1), (6, 2), (7, 2), (6, 3), (7, 3)]
GAMMA = 0.97
LIM = 1.0 / GAMMA


def tile_ensemblequantilehuberheadweightgrad_d1p_kernel(
    tc, h, hn_bytes, hn_scale, w_words, w_scales, wt_words, wt_scales, r, a, c, out
):
    nc = tc.nc
    with ExitStack() as ctx:
        ctx.enter_context(nc.allow_non_contiguous_dma(reason="small per-row vectors"))
        keep = ctx.enter_context(tc.tile_pool(name="keep", bufs=1))
        work = ctx.enter_context(tc.tile_pool(name="work", bufs=2))
        units = ctx.enter_context(tc.tile_pool(name="units", bufs=4))
        psum = ctx.enter_context(tc.psum_pool(name="psum", bufs=2))
        ctx.enter_context(tc.manual_schedule())

        w_sc = keep.tile([P, M], U8, name="w_sc", align_bytes=64)
        wt_sc = keep.tile([P, M], U8, name="wt_sc", align_bytes=64)
        nc.vector.memset(wt_sc[:].bitcast(I32), 0)
        nc.vector.memset(w_sc[:].bitcast(I32), 0)
        dummy = keep.tile([P, 1], F32, name="dummy")
        nc.vector.memset(dummy[:], 0.0)
        dummy2 = keep.tile([P, 1], F32, name="dummy2")
        ident = keep.tile([P, P], F32, name="ident", align_bytes=64)
        make_identity(nc, ident[:])
        iota_t = keep.tile([P, 1], I32, name="iota_t")
        nc.gpsimd.iota(out=iota_t[:], pattern=[[0, 1]], base=0, channel_multiplier=1)

        hv = h.rearrange("(g p t) f -> g t p f", p=P, t=4)
        hnv = hn_bytes.rearrange("(g p t) f -> g t p f", p=P, t=4)
        h_raw = [keep.tile([P, 4, D], BF16, name="h_raw%d" % g, align_bytes=64) for g in range(G)]
        hn_raw = [keep.tile([P, D], U8, name="hn_raw%d" % n, align_bytes=64) for n in range(TILES)]
        hn_sc = keep.tile([P, G, 4, 8], F32, name="hn_sc")
        w_sb = keep.tile([P, G, M], U32, name="w_sb", align_bytes=64)
        wt_sb = keep.tile([P, G, M], U32, name="wt_sb", align_bytes=64)
        r_bf = keep.tile([P, G, 4], BF16, name="r_bf")
        a_bf = keep.tile([P, G, 4], BF16, name="a_bf")
        c_bf = keep.tile([P, G, 4], BF16, name="c_bf")

        def load_tile(n):
            nc.sync.dma_start(out=hn_raw[n][:], in_=hnv[n // 4, n % 4])
            nc.sync.dma_start(out=h_raw[n // 4][:, n % 4, :], in_=hv[n // 4, n % 4])

        nc.scalar.activation(out=dummy2[:], in_=dummy[:], func=ACT.Relu)
        nc.sync.dma_start(out=hn_sc[:], in_=hn_scale.rearrange("(g p t) q -> p g t q", p=P, t=4))
        load_tile(0)
        for words, scal, w_in, s_in in ((w_sb, w_sc, w_words, w_scales), (wt_sb, wt_sc, wt_words, wt_scales)):
            for g in range(G):
                nc.sync.dma_start(out=words[:, g, :].bitcast(I32), in_=w_in[g].rearrange("p n t -> p (n t)").bitcast(I32))
            for q in range(4):
                nc.sync.dma_start(out=scal[32 * q : 32 * q + 8, :].bitcast(I32), in_=s_in[:, 4 * q : 4 * q + 4, :].bitcast(I32))
        nc.sync.dma_start(out=r_bf[:], in_=r.rearrange("(g p t) -> p g t", p=P, t=4))
        load_tile(1)
        nc.sync.dma_start(out=a_bf[:], in_=a.rearrange("(g p t) -> p g t", p=P, t=4))
        nc.sync.dma_start(out=c_bf[:], in_=c.rearrange("(g p t) -> p g t", p=P, t=4))
        for n in range(2, TILES):
            load_tile(n)

        i_int = keep.tile([P, 1], I32, name="i_int")
        i_f = keep.tile([P, 1], F32, name="i_f")
        alpha = keep.tile([P, 1], F32, name="alpha")
        beta = keep.tile([P, 1], F32, name="beta")
        neg_r = keep.tile([P, G * 4], F32, name="neg_r")
        a_f = keep.tile([P, G * 4], F32, name="a_f")
        c_f = keep.tile([P, G * 4], F32, name="c_f")

        hn_bf = {}
        codes = {}
        cscal = {}
        grp = {}
        tr_ps = {}
        th = {}
        y_ps = {}

        def widen(n, eng, blocks):
            if n not in hn_bf:
                t = work.tile([P, D], BF16, name="hn_bf", bufs=3, align_bytes=64)
                hn_bf[n] = t
            for q in blocks:
                cols = slice(128 * q, 128 * q + 128)
                src = hn_raw[n][:, cols].bitcast(FP8)
                scale = hn_sc[:, n // 4, n % 4, q : q + 1]
                if eng == "v":
                    nc.vector.tensor_scalar(out=hn_bf[n][:, cols], in0=src, scalar1=scale, scalar2=None, op0=ALU.mult)
                else:
                    nc.scalar.activation(out=hn_bf[n][:, cols], in_=src, func=ACT.Copy, scale=scale)

        def transposes(n, which):
            if which == 0:
                words = h_raw[n // 4][:, n % 4, :].bitcast(F32)
            else:
                words = hn_bf[n][:].bitcast(F32)
            wk = psum.tile([P, 4, P], F32, name="wk")
            tr_ps[n, which] = wk
            for s in range(2):
                for u in range(2):
                    nc.tensor.transpose(wk[:, 2 * s + u, :], words[:, 256 * s + u : 256 * (s + 1) : 2], ident[:])

        def evac(n, which, eng):
            if n not in grp:
                gt_ = work.tile([P, 2, 2, P, 2], F32, name="grp", bufs=3, align_bytes=64)
                grp[n] = gt_
            dst = grp[n][:, which]
            src = tr_ps[n, which][:].rearrange("p (s u) r -> p s r u", u=2)
            if eng == "v":
                nc.vector.tensor_copy(out=dst, in_=src)
            else:
                nc.scalar.copy(out=dst, in_=src)

        def quant(n, parts):
            if n not in codes:
                cd = work.tile([P, 2, 2 * P], U32, name="codes", bufs=3, align_bytes=64)
                cs = work.tile([P, 2, 2 * P], U8, name="cscal", bufs=3, align_bytes=64)
                codes[n], cscal[n] = cd, cs
            cd, cs = codes[n], cscal[n]
            nc.vector.quantize_mx(
                out=cd[:, parts, :].rearrange("p w r -> p (w r)").bitcast(FP8X4),
                scales=cs[:, parts, :].rearrange("p w r -> p (w r)"),
                in_=grp[n][:, parts].rearrange("p w s r u -> p (w s r u)").bitcast(BF16),
            )

        def mm(n, which):
            if which == 0:
                o = psum.tile([P, M], F32, name="wk")
                words, sc = w_sb, w_sc
                tr_ps[n, "th"] = o
            else:
                o = psum.tile([P, M], F32, name="y")
                words, sc = wt_sb, wt_sc
                y_ps[n] = o
            for s in range(2):
                nc.tensor.matmul_mx(
                    out=o[:],
                    lhsT=codes[n][:, which, P * s : P * s + P].bitcast(FP8X4),
                    lhsT_scale=cscal[n][:, which, P * s : P * s + P],
                    rhs=words[:, s, :].bitcast(FP8X4),
                    rhs_scale=sc[4 * s : P, :],
                    start=(s == 0),
                    stop=(s == 1),
                )

        def ev_theta(n):
            t = work.tile([P, M], F32, name="th", bufs=3, align_bytes=64)
            th[n] = t
            nc.scalar.activation(out=t[:], in_=tr_ps[n, "th"][:], func=ACT.Identity, bias=neg_r[:, n : n + 1], scale=LIM)

        dd = {}
        pp = {}
        sc_ps = {}
        sp_ps = {}

        def stage_a(u, j0=0, j1=16):
            n, cb = SEQ[u]
            if j0 == 0:
                t = units.tile([P, 16, P], F32, name="dd", bufs=5, align_bytes=64)
                dd[u] = t
            cols = slice(P * cb, P * cb + P)
            yv = y_ps[n][:, cols].rearrange("p (k j) -> p j k", j=16)[:, j0:j1, :].unsqueeze(3).to_broadcast([P, j1 - j0, 8, 16])
            tv = th[n][:, cols].rearrange("p (k i) -> p k i", i=16).unsqueeze(1).to_broadcast([P, j1 - j0, 8, 16])
            nc.vector.tensor_tensor(out=dd[u][:, j0:j1, :].rearrange("p j (k i) -> p j k i", i=16), in0=yv, in1=tv, op=ALU.subtract)

        def stage_b(u, j0=0, j1=16):
            nc.vector.tensor_scalar(out=dd[u][:, j0:j1, :], in0=dd[u][:, j0:j1, :], scalar1=-LIM, scalar2=LIM, op0=ALU.max, op1=ALU.min)

        def stage_d(u, eng="s", j0=0, j1=16):
            if j0 == 0:
                t = units.tile([P, 16, P], F32, name="pp", bufs=4, align_bytes=64)
                pp[u] = t
            dst, src = pp[u][:, j0:j1, :], dd[u][:, j0:j1, :]
            if eng == "s":
                nc.scalar.activation(out=dst, in_=src, func=ACT.Relu)
            else:
                nc.vector.tensor_scalar(out=dst, in0=src, scalar1=0.0, scalar2=None, op0=ALU.max)

        def sums(u, src, store, nm, j0=0, j1=16):
            n, cb = SEQ[u]
            key = n if n < 6 else ("pair", cb)
            x = cb if n < 6 else n - 6
            if x == 0 and j0 == 0:
                o = psum.tile([P, M if n < 6 else 2 * P], F32, name=nm)
                store[key] = o
            dst = store[key][:, P * x : P * x + P]
            for j in range(j0, j1):
                nc.tensor.matmul(out=dst, lhsT=src[u][:, j, :], rhs=ident[:], start=(j == 0), stop=(j == 15), is_transpose=True)

        gs = {}
        gb = {}
        ec = {}

        def post1(key, width, which):
            store, fac = (sc_ps, alpha) if which == 0 else (sp_ps, beta)
            t = work.tile([P, width], F32, name="gs%d" % which, align_bytes=64)
            gs[key, which] = t
            nc.scalar.activation(out=t[:], in_=store[key][:], func=ACT.Copy, scale=fac[:, 0:1])

        def post3(key, width):
            wk = psum.tile([P, width], F32, name="wk")
            gb[key] = wk
            for x in range(width // P):
                cols = slice(P * x, P * x + P)
                for which in range(2):
                    nc.tensor.matmul(out=wk[:, cols], lhsT=gs[key, which][:, cols], rhs=ident[:], start=(which == 0), stop=(which == 1), is_transpose=True)

        def post4(key, n, cols, src):
            g, t = n // 4, n % 4
            if g not in ec:
                e_ = work.tile([P, 4, M], BF16, name="ec", align_bytes=64)
                ec[g] = e_
            nc.scalar.activation(out=ec[g][:, t, cols], in_=gb[key][:, src], func=ACT.Copy, scale=c_f[:, n : n + 1])

        e_in = {}
        e_codes = {}
        e_scal = {}
        ha = {}
        ha_codes = {}
        ha_scal = {}

        def e_interleave(g, cols, eng):
            if g not in e_in:
                t = work.tile([P, M, 4], BF16, name="e_in", align_bytes=64)
                e_in[g] = t
            (nc.vector.tensor_copy if eng == "v" else nc.scalar.copy)(out=e_in[g][:, cols, :], in_=ec[g][:, :, cols].rearrange("p t m -> p m t"))

        def e_quant(g, cols):
            if g not in e_codes:
                cd = keep.tile([P, M], U32, name="e_codes%d" % g, align_bytes=64)
                cs = keep.tile([P, M], U8, name="e_scal%d" % g, align_bytes=64)
                e_codes[g], e_scal[g] = cd, cs
            nc.vector.quantize_mx(out=e_codes[g][:, cols].bitcast(FP8X4), scales=e_scal[g][:, cols], in_=e_in[g][:, cols, :].rearrange("p m t -> p (m t)"))

        def ha_chunk(x):
            g, f0 = x // 8, 128 * (x % 8)
            if x % 8 == 0:
                t = keep.tile([P, D, 4], BF16, name="ha%d" % g, align_bytes=64)
                ha[g] = t
            f = slice(f0, f0 + 128)
            ac = work.tile([P, 4], F32, name="ac", bufs=3)
            nc.vector.tensor_copy(out=ac[:], in_=a_f[:, 4 * g : 4 * g + 4])
            nc.gpsimd.tensor_tensor(
                out=ha[g][:, f, :],
                in0=h_raw[g][:, :, f].rearrange("p t f -> p f t"),
                in1=ac[:].unsqueeze(1).to_broadcast([P, 128, 4]),
                op=ALU.mult,
            )

        def ha_quant(g, half):
            if half == 0:
                cd = keep.tile([P, D], U32, name="ha_codes%d" % g, align_bytes=64)
                cs = keep.tile([P, D], U8, name="ha_scal%d" % g, align_bytes=64)
                ha_codes[g], ha_scal[g] = cd, cs
            f = slice(512 * half, 512 * half + 512)
            nc.vector.quantize_mx(out=ha_codes[g][:, f].bitcast(FP8X4), scales=ha_scal[g][:, f], in_=ha[g][:, f, :].rearrange("p f t -> p (f t)"))

        out_v = out.rearrange("(m p) c -> p m c", p=P)

        def dw_part(x, part, tag, eng):
            cols = slice(2 * P * x, 2 * P * x + 2 * P)
            o = psum.tile([P, 2, 2 * P], F32, name=tag)
            for y in range(2):
                f = slice(P * (2 * part + y), P * (2 * part + y) + P)
                for g in range(G):
                    nc.tensor.matmul_mx(
                        out=o[:, y, :],
                        lhsT=ha_codes[g][:, f].bitcast(FP8X4),
                        lhsT_scale=ha_scal[g][:, f],
                        rhs=e_codes[g][:, cols].bitcast(FP8X4),
                        rhs_scale=e_scal[g][:, cols],
                        start=(g == 0),
                        stop=(g == G - 1),
                    )
            t = work.tile([P, 2, 2 * P], F32, name="res", bufs=8, align_bytes=64)
            if eng == "v":
                nc.vector.tensor_copy(out=t[:], in_=o[:])
            else:
                nc.scalar.copy(out=t[:], in_=o[:])
            nc.sync.dma_start(out=out_v[:, 2 * part : 2 * part + 2, cols], in_=t[:])

        def e_block(x):
            e_interleave(1, slice(2 * P * x, 2 * P * x + 2 * P), "v")
            e_quant(1, slice(2 * P * x, 2 * P * x + 2 * P))

        def pair_post1(cb, which):
            post1(("pair", cb), 2 * P, which)

        def pair_post3(cb):
            post3(("pair", cb), 2 * P)

        def pair_post4(cb):
            cols = slice(P * cb, P * cb + P)
            post4(("pair", cb), 6, cols, slice(0, P))
            post4(("pair", cb), 7, cols, slice(P, 2 * P))

        widen(0, "v", range(0, 5))
        widen(0, "s", range(5, 8))
        transposes(0, 0)
        evac(0, 0, "v")
        transposes(0, 1)
        evac(0, 1, "s")
        quant(0, slice(0, 1))
        quant(0, slice(1, 2))
        nc.vector.tensor_scalar(out=neg_r[:], in0=r_bf[:].rearrange("p g t -> p (g t)"), scalar1=-LIM, scalar2=None, op0=ALU.mult)
        mm(0, 0)
        ev_theta(0)
        mm(0, 1)
        widen(1, "s", range(8))

        n_units = 4 * TILES
        chunk_slots = [s for s in range(2, 24) if s % 4 != 0][:16]
        for s in range(n_units):
            n, ph = s // 4, s % 4
            if s in chunk_slots:
                ha_chunk(chunk_slots.index(s))
            stage_a(s, 0, 8 if s == n_units - 1 else 16)
            if s == 0:
                transposes(1, 0)
                evac(1, 0, "v")
                transposes(1, 1)
                evac(1, 1, "s")
                nc.vector.tensor_scalar(out=i_int[:], in0=iota_t[:], scalar1=15, scalar2=None, op0=ALU.bitwise_and)
                nc.vector.tensor_copy(out=i_f[:], in_=i_int[:])
                nc.scalar.copy(out=a_f[:], in_=a_bf[:].rearrange("p g t -> p (g t)"))
                nc.scalar.copy(out=c_f[:], in_=c_bf[:].rearrange("p g t -> p (g t)"))
                widen(2, "s", range(0, 4))
            if s == 1:
                nc.vector.tensor_scalar(out=alpha[:], in0=i_f[:], scalar1=2.0 * GAMMA / 16384.0, scalar2=-31.0 * GAMMA / 16384.0, op0=ALU.mult, op1=ALU.add)
                nc.vector.tensor_scalar(out=beta[:], in0=i_f[:], scalar1=-2.0 * GAMMA / 8192.0, scalar2=15.0 * GAMMA / 8192.0, op0=ALU.mult, op1=ALU.add)
            if ph == 0 and n + 1 < TILES:
                quant(n + 1, slice(0, 2))
            if s in (15, 18):
                ha_quant(0, (s - 15) // 3)
            if s >= 1:
                stage_b(s - 1)
                stage_d(s - 1)
            if ph == 1 and n + 2 < TILES:
                transposes(n + 2, 0)
            if ph == 2 and n + 2 < TILES:
                transposes(n + 2, 1)
            if s >= 2:
                sums(s - 2, pp, sp_ps, "sp")
            if ph == 0 and n + 1 < TILES:
                mm(n + 1, 0)
                mm(n + 1, 1)
            if ph == 3 and 1 <= n <= TILES - 2:
                post3(n - 1, M)
            for u in (26, 27):
                if s == u + 3:
                    pair_post3(SEQ[u][1])
            if s >= 1:
                sums(s - 1, dd, sc_ps, "sc")
            if ph == 0:
                if n + 1 < TILES:
                    ev_theta(n + 1)
                if n + 2 < TILES:
                    widen(n + 2, "s", range(4, 8))
            if ph == 1:
                if n + 2 < TILES:
                    evac(n + 2, 0, "s")
                if 1 <= n <= TILES - 2:
                    post1(n - 1, M, 0)
            if ph == 2:
                if n + 2 < TILES:
                    evac(n + 2, 1, "s")
                if 1 <= n <= TILES - 2:
                    post1(n - 1, M, 1)
            if ph == 3:
                if n + 3 < TILES:
                    widen(n + 3, "s", range(0, 4))
                if 1 <= n <= TILES - 2:
                    post4(n - 1, n - 1, slice(0, M), slice(0, M))
            if s == 22:
                e_interleave(0, slice(0, M), "s")
            for u in (26, 27, 29):
                if s == u + 2:
                    pair_post1(SEQ[u][1], 0)
                    pair_post1(SEQ[u][1], 1)
            for u in (26, 27):
                if s == u + 3:
                    pair_post4(SEQ[u][1])

        stage_b(31, 0, 8)
        sums(31, dd, sc_ps, "sc", 0, 8)
        stage_a(31, 8, 16)
        stage_d(31, "v", 0, 8)
        stage_b(31, 8, 16)
        sums(31, dd, sc_ps, "sc", 8, 16)
        stage_d(31, "v", 8, 16)
        sums(30, pp, sp_ps, "sp")
        sums(31, pp, sp_ps, "sp")
        e_quant(0, slice(0, M))
        ha_quant(1, 0)
        ha_quant(1, 1)
        e_block(0)
        pair_post1(3, 0)
        pair_post3(2)
        pair_post1(3, 1)
        pair_post4(2)
        pair_post3(3)
        pair_post4(3)
        for part, tag, eng in ((0, "y", "v"), (1, "y", "s"), (2, "sc", "v"), (3, "sp", "s")):
            dw_part(0, part, tag, eng)
            if part == 0:
                e_block(1)
        for part, tag, eng in ((0, "y", "s"), (1, "y", "v"), (2, "sc", "s"), (3, "sp", "v")):
            dw_part(1, part, tag, eng)
